import numpy as np
import ml_dtypes


def mxq(x, axis, fmt="e4m3"):
    dtype, down = {"e4m3": (ml_dtypes.float8_e4m3fn, 7), "e5m2": (ml_dtypes.float8_e5m2, 14)}[fmt]
    v = np.moveaxis(np.asarray(x, np.float32).astype(ml_dtypes.bfloat16).astype(np.float64), axis, -1)
    blocks = v.reshape(v.shape[:-1] + (-1, 32))
    amax = np.abs(blocks).max(-1, keepdims=True)
    byte = np.maximum(np.where(amax > 0, np.frexp(amax)[1] - 1 + 127, 0) - down, 1)
    scale = np.exp2(byte - 127.0)
    codes = (blocks / scale).astype(np.float32).astype(dtype).astype(np.float64)
    return np.moveaxis((codes * scale).reshape(v.shape), -1, axis)


WIDE = False


def mx_kscale(k):
    if not WIDE:
        return np.ones(k)
    levels = np.array([10, -10, 5, -5, 0])
    if k % 512:
        return np.exp2(np.random.permutation(np.resize(levels, k // 32))).repeat(32)
    a = np.empty((k // 512, 16))
    for p in range(k // 512):
        a[p, :8] = np.random.permutation(np.resize(levels, 8))
        for g in range(8):
            far = levels[np.abs(levels - a[p, g]) >= 10]
            a[p, g + 8] = far[np.random.randint(len(far))]
    return np.exp2(a.ravel()).repeat(32)


def f64(x):
    return np.asarray(x).astype(np.float64)


def striped(idx):
    return np.tile(idx.reshape(-1, 16).T, (8, 1)).astype(np.uint16)


def unstriped(offs):
    return offs[:16].T.reshape(-1).astype(np.int64)


def pack_weight(w):
    k, n = w.shape
    w = f64(np.asarray(w, np.float32).astype(ml_dtypes.bfloat16)).reshape(k // 32, 32, n)
    amax = np.abs(w).max(1)
    byte = np.clip(np.where(amax > 0, np.frexp(amax)[1] - 1 + 127 - 7, 1), 1, 254)
    scaled = (w * np.exp2(127.0 - byte)[:, None, :]).reshape(k, n).astype(np.float32)
    words = np.ascontiguousarray(scaled.reshape(k // 512, 128, 4, n).transpose(0, 1, 3, 2)).astype(ml_dtypes.float8_e4m3fn).view(np.uint8)
    return words, np.ascontiguousarray(byte.astype(np.uint8).reshape(k // 512, 16, n))


def unpack_weight(words, scales):
    g, p, n, _ = words.shape
    vals = np.ascontiguousarray(words).view(ml_dtypes.float8_e4m3fn).astype(np.float64) * np.repeat(np.exp2(scales.astype(np.float64) - 127.0), 8, axis=1)[..., None]
    return vals.transpose(0, 1, 3, 2).reshape(g * 512, n)


E2M1 = np.array([0.0, 0.5, 1.0, 1.5, 2.0, 3.0, 4.0, 6.0, -0.0, -0.5, -1.0, -1.5, -2.0, -3.0, -4.0, -6.0])


def pack_fp4(w):
    k, n = w.shape
    w = f64(np.asarray(w, np.float32).astype(ml_dtypes.bfloat16)).reshape(k // 32, 32, n)
    amax = np.abs(w).max(1)
    mant, ex = np.frexp(amax / 6.0)
    byte = np.clip(np.where(amax > 0, np.where(mant > 0.5, ex, ex - 1) + 127, 1), 1, 254)
    scaled = (w * np.exp2(127.0 - byte)[:, None, :]).reshape(k, n).astype(np.float32)
    c = np.ascontiguousarray(scaled.reshape(k // 512, 128, 4, n).transpose(0, 1, 3, 2)).astype(ml_dtypes.float4_e2m1fn).view(np.uint8) & 0xF
    words = (c[..., 0::2] | (c[..., 1::2] << 4)).reshape(k // 512, 128, 2 * n)
    return np.ascontiguousarray(words), np.ascontiguousarray(byte.astype(np.uint8).reshape(k // 512, 16, n))


def unpack_fp4(words, scales):
    g, _, n = scales.shape
    words = np.ascontiguousarray(words).reshape(g, 128, n, 2)
    nib = np.empty((g, 128, n, 4), np.uint8)
    nib[..., 0::2] = words & 0xF
    nib[..., 1::2] = words >> 4
    vals = E2M1[nib] * np.repeat(np.exp2(scales.astype(np.float64) - 127.0), 8, axis=1)[..., None]
    return vals.transpose(0, 1, 3, 2).reshape(g * 512, n)


def silu(v):
    return v / (1.0 + np.exp(-np.maximum(v, -700.0)))


K, T, S, V, H, N, J = 1024, 2048, 1024, 512, 512, 128, 512


def setup_inputs():
    n = np.random.standard_normal
    s = mx_kscale(K)[:, None]
    u = mx_kscale(H)
    r = mx_kscale(J)[:, None]
    packed_xT = pack_weight(n((K, T)) * s)
    packed_w4 = pack_fp4(n((H, N)) / np.sqrt(H) / u[:, None])
    return {
        "x_words": packed_xT[0],
        "x_scales": packed_xT[1],
        "eT": (n((J, V)) * r).astype(np.float32),
        "w1": (n((K, H)) / np.sqrt(3 * K) / s * u).astype(np.float32),
        "w2": (n((K, H)) / np.sqrt(3 * K) / s * u).astype(np.float32),
        "w3": (n((J, H)) / np.sqrt(3 * J) / r * u).astype(np.float32),
        "w4_words": packed_w4[0],
        "w4_scales": packed_w4[1],
        "offs": striped(np.random.permutation(T)[:S]),
    }


def reference(x_words, x_scales, eT, w1, w2, w3, w4_words, w4_scales, offs):
    xq = unpack_weight(x_words, x_scales)[:, unstriped(offs)]
    h = silu(mxq(f64(w1), 0, "e4m3").T @ xq[:, :V] + mxq(f64(w2), 0, "e4m3").T @ xq[:, V:2 * V] + mxq(f64(w3), 0, "e4m3").T @ mxq(f64(eT), 0, "e4m3"))
    return unpack_fp4(w4_words, w4_scales).T @ mxq(h, 0, "e4m3")

@@ -1,0 +1,167 @@
+from contextlib import ExitStack
+
+import concourse.mybir as mybir
+
+K, T, S, V, H, N, J = 1024, 2048, 1024, 512, 512, 128, 512
+FLOPS = 2 * (2 * K * H * V + J * H * V + H * N * V)
+
+F32 = mybir.dt.float32
+BF16 = mybir.dt.bfloat16
+I32 = mybir.dt.int32
+U32 = mybir.dt.uint32
+U16 = mybir.dt.uint16
+U8 = mybir.dt.uint8
+FP8X4 = mybir.dt.float8_e4m3fn_x4
+FP4X4 = mybir.dt.float4_e2m1fn_x4
+SILU = mybir.ActivationFunctionType.Silu
+
+P = 128
+PACK = 4
+K_PASS = P * PACK
+CHUNK = 128
+CHUNKS = V // CHUNK
+M_SCALAR = (128, 80, 64, 64, 56)
+E_LOADS = ((0, 256), (256, 384), (384, 512))
+
+
+def tile_picked_edgeup_silu_p_kernel(
+    tc, x_words, x_scales, eT, w1, w2, w3, w4_words, w4_scales, offs, out
+):
+    nc = tc.nc
+    with ExitStack() as ctx:
+        keep = ctx.enter_context(tc.tile_pool(name="keep", bufs=1))
+        psum = ctx.enter_context(tc.psum_pool(name="psum", bufs=1))
+
+        offsets = keep.tile([P, S // 16], U16, name="offsets")
+        nc.sync.dma_start(offsets[:], offs)
+
+        x_scale_table = keep.tile([P, T], U8, name="x_scale_table", align_bytes=64)
+        nc.vector.memset(x_scale_table[:].bitcast(I32), 0)
+
+        zero = keep.tile([P, 1], F32, name="zero")
+        nc.vector.memset(zero[:], 0.0)
+        silu_bias = keep.tile([P, 1], F32, name="silu_bias")
+        nc.scalar.activation(silu_bias[:], zero[:], SILU)
+
+        w4_codes = keep.tile([P, 2 * N], U8, name="w4_codes", align_bytes=64)
+        w4_plane = keep.tile([P, N], U8, name="w4_plane", align_bytes=64)
+        nc.gpsimd.memset(w4_plane[:].bitcast(I32), 0)
+
+        def load_table(z):
+            table = keep.tile([P, T], I32, name="x_table%d" % z, align_bytes=64)
+            nc.sync.dma_start(out=table[:], in_=x_words[z].rearrange("p n t -> p (n t)").bitcast(I32))
+            return table
+
+        def load_weights(i, rows):
+            raw = keep.tile([P, PACK, H], F32, name="w_raw%d" % i)
+            nc.sync.dma_start(out=raw[:], in_=rows.rearrange("(p j) c -> p j c", j=PACK))
+            return raw
+
+        weight_rows = [w1[0:K_PASS], w2[0:K_PASS], w1[K_PASS:K], w2[K_PASS:K], w3]
+        x_tables = [load_table(0)]
+        for q in range(4):
+            nc.sync.dma_start(
+                out=x_scale_table[32 * q : 32 * q + 8, :].bitcast(I32),
+                in_=x_scales[:, 4 * q : 4 * q + 4, :].bitcast(I32),
+            )
+        raw_weights = [load_weights(0, weight_rows[0])]
+        x_tables.append(load_table(1))
+        nc.sync.dma_start(out=w4_codes[:].bitcast(I32), in_=w4_words[0].bitcast(I32))
+        for q in range(4):
+            nc.sync.dma_start(
+                out=w4_plane[32 * q : 32 * q + 4, :].bitcast(I32),
+                in_=w4_scales[0, 4 * q : 4 * q + 4, :].bitcast(I32),
+            )
+        for i in range(1, 5):
+            raw_weights.append(load_weights(i, weight_rows[i]))
+
+        e_view = eT.rearrange("(p j) v -> p j v", j=PACK)
+        raw_edges = []
+        for lo, hi in E_LOADS:
+            raw = keep.tile([P, PACK, hi - lo], F32, name="e_raw%d" % lo)
+            nc.sync.dma_start(out=raw[:], in_=e_view[:, :, lo:hi])
+            for v0 in range(lo, hi, CHUNK):
+                raw_edges.append(raw[:, :, v0 - lo : v0 - lo + CHUNK])
+
+        x_plane = keep.tile([P, S], U8, name="x_plane", align_bytes=64)
+        x_codes = []
+        for z in range(2):
+            picked = keep.tile([P, S], U32, name="x_codes%d" % z, align_bytes=64)
+            nc.vector.tensor_copy(picked[:], x_tables[z][:].bitcast(U32).indirect(offsets[:]))
+            x_codes.append(picked)
+            if z == 0:
+                nc.vector.tensor_copy(x_plane[:], x_scale_table[:].indirect(offsets[:]))
+
+        banks = [psum.tile([P, PACK, CHUNK], F32, name="h_bank%d" % c) for c in range(CHUNKS)]
+
+        def quantize_weights(i):
+            grouped = keep.tile([P, H * PACK], BF16, name="w_grouped%d" % i, align_bytes=64)
+            src = raw_weights[i][:].rearrange("p j (m t) -> p m t j", t=PACK)
+            dst = grouped[:].rearrange("p (t m j) -> p m t j", t=PACK, j=PACK)
+            split = M_SCALAR[i]
+            nc.scalar.copy(dst[:, :split], src[:, :split])
+            if split < P:
+                nc.vector.tensor_copy(dst[:, split:], src[:, split:])
+            codes = keep.tile([P, H], U32, name="w_codes%d" % i, align_bytes=64)
+            plane = keep.tile([P, H], U8, name="w_plane%d" % i, align_bytes=64)
+            nc.vector.quantize_mx(out=codes[:].bitcast(FP8X4), scales=plane[:], in_=grouped[:])
+            return codes, plane
+
+        def add_pass(c, weights, rhs, rhs_scale, first, last):
+            codes, plane = weights
+            for t in range(PACK):
+                cols = slice(t * P, (t + 1) * P)
+                nc.tensor.matmul_mx(
+                    out=banks[c][:, t, :],
+                    lhsT=codes[:, cols].bitcast(FP8X4),
+                    lhsT_scale=plane[:, cols],
+                    rhs=rhs.bitcast(FP8X4),
+                    rhs_scale=rhs_scale,
+                    start=(first and t == 0),
+                    stop=(last and t == PACK - 1),
+                )
+
+        for i in range(4):
+            z, side = divmod(i, 2)
+            weights = quantize_weights(i)
+            for c in range(CHUNKS):
+                cols = slice(side * V + c * CHUNK, side * V + (c + 1) * CHUNK)
+                add_pass(c, weights, x_codes[z][:, cols], x_plane[4 * z : P, cols], i == 0, False)
+
+        edge_weights = quantize_weights(4)
+
+        def quantize_columns(name, grouped):
+            codes = keep.tile([P, CHUNK], U32, name=name + "_codes", align_bytes=64)
+            plane = keep.tile([P, CHUNK], U8, name=name + "_plane", align_bytes=64)
+            nc.vector.quantize_mx(out=codes[:].bitcast(FP8X4), scales=plane[:], in_=grouped[:])
+            return codes, plane
+
+        for c in range(CHUNKS):
+            e_grouped = keep.tile([P, CHUNK * PACK], BF16, name="e_grouped%d" % c, align_bytes=64)
+            nc.vector.tensor_copy(
+                e_grouped[:].rearrange("p (v j) -> p v j", j=PACK), raw_edges[c].rearrange("p j v -> p v j")
+            )
+            e_codes, e_plane = quantize_columns("e%d" % c, e_grouped)
+            add_pass(c, edge_weights, e_codes[:], e_plane[:], False, True)
+
+            h_grouped = keep.tile([P, CHUNK * PACK], BF16, name="h_grouped%d" % c, align_bytes=64)
+            nc.scalar.activation(
+                h_grouped[:].rearrange("p (v t) -> p v t", t=PACK),
+                banks[c][:].rearrange("p t v -> p v t"),
+                SILU,
+                bias=silu_bias[:],
+            )
+            h_codes, h_plane = quantize_columns("h%d" % c, h_grouped)
+            out_bank = psum.tile([P, CHUNK], F32, name="out_bank%d" % c)
+            nc.tensor.matmul_mx(
+                out=out_bank[:],
+                lhsT=w4_codes[:].bitcast(FP4X4),
+                lhsT_scale=w4_plane[:],
+                rhs=h_codes[:].bitcast(FP8X4),
+                rhs_scale=h_plane[:],
+                start=True,
+                stop=True,
+            )
+            result = keep.tile([P, CHUNK], F32, name="result%d" % c)
+            nc.scalar.copy(result[:], out_bank[:])
+            nc.sync.dma_start(out=out[:, c * CHUNK : (c + 1) * CHUNK], in_=result[:])

@@ -20,8 +20,11 @@ PACK = 4
 K_PASS = P * PACK
 CHUNK = 128
 CHUNKS = V // CHUNK
-M_SCALAR = (128, 80, 64, 64, 56)
+HALF = P // 2
+E_SLOTS = ((0, 0), (0, 1), (1, 0), (0, 1))
 E_LOADS = ((0, 256), (256, 384), (384, 512))
+E_ON_SCALAR = (1,)
+OUT_GROUPS = ((0, 2, False), (2, 3, False), (3, 4, True))
 
 
 def tile_picked_edgeup_silu_p_kernel(
@@ -37,34 +40,32 @@ def tile_picked_edgeup_silu_p_kernel(
 
         x_scale_table = keep.tile([P, T], U8, name="x_scale_table", align_bytes=64)
         nc.vector.memset(x_scale_table[:].bitcast(I32), 0)
+        w4_codes = keep.tile([P, 2 * N], U8, name="w4_codes", align_bytes=64)
+        w4_plane = keep.tile([P, N], U8, name="w4_plane", align_bytes=64)
+        nc.vector.memset(w4_plane[:].bitcast(I32), 0)
 
         zero = keep.tile([P, 1], F32, name="zero")
         nc.vector.memset(zero[:], 0.0)
         silu_bias = keep.tile([P, 1], F32, name="silu_bias")
         nc.scalar.activation(silu_bias[:], zero[:], SILU)
 
-        w4_codes = keep.tile([P, 2 * N], U8, name="w4_codes", align_bytes=64)
-        w4_plane = keep.tile([P, N], U8, name="w4_plane", align_bytes=64)
-        nc.gpsimd.memset(w4_plane[:].bitcast(I32), 0)
-
         def load_table(z):
             table = keep.tile([P, T], I32, name="x_table%d" % z, align_bytes=64)
             nc.sync.dma_start(out=table[:], in_=x_words[z].rearrange("p n t -> p (n t)").bitcast(I32))
             return table
 
-        def load_weights(i, rows):
-            raw = keep.tile([P, PACK, H], F32, name="w_raw%d" % i)
-            nc.sync.dma_start(out=raw[:], in_=rows.rearrange("(p j) c -> p j c", j=PACK))
+        def load_columns(name, rows, lo, hi):
+            raw = keep.tile([P, PACK, hi - lo], F32, name="%s_raw%d" % (name, lo))
+            nc.sync.dma_start(out=raw[:], in_=rows.rearrange("(p j) c -> p j c", j=PACK)[:, :, lo:hi])
             return raw
 
-        weight_rows = [w1[0:K_PASS], w2[0:K_PASS], w1[K_PASS:K], w2[K_PASS:K], w3]
         x_tables = [load_table(0)]
         for q in range(4):
             nc.sync.dma_start(
                 out=x_scale_table[32 * q : 32 * q + 8, :].bitcast(I32),
                 in_=x_scales[:, 4 * q : 4 * q + 4, :].bitcast(I32),
             )
-        raw_weights = [load_weights(0, weight_rows[0])]
+        raw_weights = [load_columns("w1a", w1[0:K_PASS], 0, H)]
         x_tables.append(load_table(1))
         nc.sync.dma_start(out=w4_codes[:].bitcast(I32), in_=w4_words[0].bitcast(I32))
         for q in range(4):
@@ -72,14 +73,13 @@ def tile_picked_edgeup_silu_p_kernel(
                 out=w4_plane[32 * q : 32 * q + 4, :].bitcast(I32),
                 in_=w4_scales[0, 4 * q : 4 * q + 4, :].bitcast(I32),
             )
-        for i in range(1, 5):
-            raw_weights.append(load_weights(i, weight_rows[i]))
-
-        e_view = eT.rearrange("(p j) v -> p j v", j=PACK)
+        raw_weights.append(load_columns("w2a", w2[0:K_PASS], 0, H))
+        raw_weights.append(load_columns("w1b", w1[K_PASS:K], 0, H))
+        raw_weights.append(load_columns("w2b", w2[K_PASS:K], 0, H))
+        raw_w3 = load_columns("w3", w3, 0, H)
         raw_edges = []
         for lo, hi in E_LOADS:
-            raw = keep.tile([P, PACK, hi - lo], F32, name="e_raw%d" % lo)
-            nc.sync.dma_start(out=raw[:], in_=e_view[:, :, lo:hi])
+            raw = load_columns("e", eT, lo, hi)
             for v0 in range(lo, hi, CHUNK):
                 raw_edges.append(raw[:, :, v0 - lo : v0 - lo + CHUNK])
 
@@ -94,21 +94,34 @@ def tile_picked_edgeup_silu_p_kernel(
 
         banks = [psum.tile([P, PACK, CHUNK], F32, name="h_bank%d" % c) for c in range(CHUNKS)]
 
-        def quantize_weights(i):
-            grouped = keep.tile([P, H * PACK], BF16, name="w_grouped%d" % i, align_bytes=64)
-            src = raw_weights[i][:].rearrange("p j (m t) -> p m t j", t=PACK)
-            dst = grouped[:].rearrange("p (t m j) -> p m t j", t=PACK, j=PACK)
-            split = M_SCALAR[i]
-            nc.scalar.copy(dst[:, :split], src[:, :split])
-            if split < P:
-                nc.vector.tensor_copy(dst[:, split:], src[:, split:])
-            codes = keep.tile([P, H], U32, name="w_codes%d" % i, align_bytes=64)
-            plane = keep.tile([P, H], U8, name="w_plane%d" % i, align_bytes=64)
-            nc.vector.quantize_mx(out=codes[:].bitcast(FP8X4), scales=plane[:], in_=grouped[:])
+        def quantize_weights(name, raw, copies):
+            codes = keep.tile([P, H], U32, name=name + "_codes", align_bytes=64)
+            plane = keep.tile([P, H], U8, name=name + "_plane", align_bytes=64)
+            src = raw[:].rearrange("p j (m t) -> p m j t", t=PACK)
+            stages = []
+            for half, copy in enumerate(copies):
+                stage = keep.tile([P, H * PACK // 2], BF16, name="%s_stage%d" % (name, half), align_bytes=64)
+                copy(stage[:].rearrange("p (t m j) -> p m j t", t=PACK, j=PACK), src[:, half * HALF : (half + 1) * HALF])
+                stages.append(stage)
+            for half, stage in enumerate(stages):
+                for t in range(PACK):
+                    cols = slice(t * P + half * HALF, t * P + (half + 1) * HALF)
+                    nc.vector.quantize_mx(
+                        out=codes[:, cols].bitcast(FP8X4),
+                        scales=plane[:, cols],
+                        in_=stage[:, t * HALF * PACK : (t + 1) * HALF * PACK],
+                    )
+            return codes, plane, stages
+
+        def quantize(name, grouped):
+            width = grouped.shape[1] // PACK
+            codes = keep.tile([P, width], U32, name=name + "_codes", align_bytes=64)
+            plane = keep.tile([P, width], U8, name=name + "_plane", align_bytes=64)
+            nc.vector.quantize_mx(out=codes[:].bitcast(FP8X4), scales=plane[:], in_=grouped)
             return codes, plane
 
         def add_pass(c, weights, rhs, rhs_scale, first, last):
-            codes, plane = weights
+            codes, plane = weights[:2]
             for t in range(PACK):
                 cols = slice(t * P, (t + 1) * P)
                 nc.tensor.matmul_mx(
@@ -121,29 +134,36 @@ def tile_picked_edgeup_silu_p_kernel(
                     stop=(last and t == PACK - 1),
                 )
 
+        shared = (nc.vector.tensor_copy, nc.scalar.copy)
+        scalar_alone = (nc.scalar.copy, nc.scalar.copy)
+        node_weights = []
         for i in range(4):
             z, side = divmod(i, 2)
-            weights = quantize_weights(i)
+            weights = quantize_weights("w%d" % i, raw_weights[i], shared if i > 0 else scalar_alone)
+            node_weights.append(weights)
             for c in range(CHUNKS):
                 cols = slice(side * V + c * CHUNK, side * V + (c + 1) * CHUNK)
                 add_pass(c, weights, x_codes[z][:, cols], x_plane[4 * z : P, cols], i == 0, False)
 
-        edge_weights = quantize_weights(4)
+        edge_weights = quantize_weights("w3", raw_w3, shared)
+        w3_stages = edge_weights[2]
 
-        def quantize_columns(name, grouped):
-            codes = keep.tile([P, CHUNK], U32, name=name + "_codes", align_bytes=64)
-            plane = keep.tile([P, CHUNK], U8, name=name + "_plane", align_bytes=64)
-            nc.vector.quantize_mx(out=codes[:].bitcast(FP8X4), scales=plane[:], in_=grouped[:])
-            return codes, plane
-
+        edge_codes = []
         for c in range(CHUNKS):
-            e_grouped = keep.tile([P, CHUNK * PACK], BF16, name="e_grouped%d" % c, align_bytes=64)
-            nc.vector.tensor_copy(
-                e_grouped[:].rearrange("p (v j) -> p v j", j=PACK), raw_edges[c].rearrange("p j v -> p v j")
-            )
-            e_codes, e_plane = quantize_columns("e%d" % c, e_grouped)
+            half, slot = E_SLOTS[c]
+            e_grouped = w3_stages[half][:, slot * CHUNK * PACK : (slot + 1) * CHUNK * PACK]
+            dst = e_grouped.rearrange("p (v i j) -> p v j i", i=PACK, j=PACK)
+            src = raw_edges[c].rearrange("p j (v i) -> p v j i", i=PACK)
+            if c in E_ON_SCALAR:
+                nc.scalar.copy(dst, src)
+            else:
+                nc.vector.tensor_copy(dst, src)
+            e_codes, e_plane = quantize("e%d" % c, e_grouped)
+            edge_codes.append(e_codes)
             add_pass(c, edge_weights, e_codes[:], e_plane[:], False, True)
 
+        hidden = []
+        for c in range(CHUNKS):
             h_grouped = keep.tile([P, CHUNK * PACK], BF16, name="h_grouped%d" % c, align_bytes=64)
             nc.scalar.activation(
                 h_grouped[:].rearrange("p (v t) -> p v t", t=PACK),
@@ -151,17 +171,26 @@ def tile_picked_edgeup_silu_p_kernel(
                 SILU,
                 bias=silu_bias[:],
             )
-            h_codes, h_plane = quantize_columns("h%d" % c, h_grouped)
-            out_bank = psum.tile([P, CHUNK], F32, name="out_bank%d" % c)
-            nc.tensor.matmul_mx(
-                out=out_bank[:],
-                lhsT=w4_codes[:].bitcast(FP4X4),
-                lhsT_scale=w4_plane[:],
-                rhs=h_codes[:].bitcast(FP8X4),
-                rhs_scale=h_plane[:],
-                start=True,
-                stop=True,
-            )
-            result = keep.tile([P, CHUNK], F32, name="result%d" % c)
-            nc.scalar.copy(result[:], out_bank[:])
-            nc.sync.dma_start(out=out[:, c * CHUNK : (c + 1) * CHUNK], in_=result[:])
+            hidden.append(quantize("h%d" % c, h_grouped[:]))
+
+        results = []
+        for lo, hi, on_scalar in OUT_GROUPS:
+            out_bank = psum.tile([P, (hi - lo) * CHUNK], F32, name="out_bank%d" % lo)
+            for c in range(lo, hi):
+                h_codes, h_plane = hidden[c]
+                nc.tensor.matmul_mx(
+                    out=out_bank[:, (c - lo) * CHUNK : (c - lo + 1) * CHUNK],
+                    lhsT=w4_codes[:].bitcast(FP4X4),
+                    lhsT_scale=w4_plane[:],
+                    rhs=h_codes[:].bitcast(FP8X4),
+                    rhs_scale=h_plane[:],
+                    start=True,
+                    stop=True,
+                )
+            result = keep.tile([P, (hi - lo) * CHUNK], F32, name="result%d" % lo)
+            if on_scalar:
+                nc.scalar.copy(result[:], out_bank[:])
+            else:
+                nc.vector.tensor_copy(result[:], out_bank[:])
+            nc.sync.dma_start(out=out[:, lo * CHUNK : hi * CHUNK], in_=result[:])
+            results.append(result)

@@ -18,12 +18,11 @@ SILU = mybir.ActivationFunctionType.Silu
 P = 128
 PACK = 4
 K_PASS = P * PACK
+QUADRANTS = 4
 CHUNK = 128
 CHUNKS = V // CHUNK
+LINE = 4
 HALF = P // 2
-E_SLOTS = ((0, 0), (0, 1), (1, 0), (0, 1))
-E_LOADS = ((0, 256), (256, 384), (384, 512))
-E_ON_SCALAR = (1,)
 OUT_GROUPS = ((0, 2, False), (2, 3, False), (3, 4, True))
 
 
@@ -34,6 +33,16 @@ def tile_picked_edgeup_silu_p_kernel(
     with ExitStack() as ctx:
         keep = ctx.enter_context(tc.tile_pool(name="keep", bufs=1))
         psum = ctx.enter_context(tc.psum_pool(name="psum", bufs=1))
+
+        def load_table(z):
+            table = keep.tile([P, T], I32, name="x_table%d" % z, align_bytes=64)
+            nc.sync.dma_start(out=table[:], in_=x_words[z].rearrange("p n t -> p (n t)").bitcast(I32))
+            return table
+
+        def load_rows(name, rows):
+            raw = keep.tile([P, PACK, rows.shape[1]], F32, name=name + "_raw")
+            nc.sync.dma_start(out=raw[:], in_=rows.rearrange("(p j) c -> p j c", j=PACK))
+            return raw
 
         offsets = keep.tile([P, S // 16], U16, name="offsets")
         nc.sync.dma_start(offsets[:], offs)
@@ -49,43 +58,29 @@ def tile_picked_edgeup_silu_p_kernel(
         silu_bias = keep.tile([P, 1], F32, name="silu_bias")
         nc.scalar.activation(silu_bias[:], zero[:], SILU)
 
-        def load_table(z):
-            table = keep.tile([P, T], I32, name="x_table%d" % z, align_bytes=64)
-            nc.sync.dma_start(out=table[:], in_=x_words[z].rearrange("p n t -> p (n t)").bitcast(I32))
-            return table
-
-        def load_columns(name, rows, lo, hi):
-            raw = keep.tile([P, PACK, hi - lo], F32, name="%s_raw%d" % (name, lo))
-            nc.sync.dma_start(out=raw[:], in_=rows.rearrange("(p j) c -> p j c", j=PACK)[:, :, lo:hi])
-            return raw
-
         x_tables = [load_table(0)]
-        for q in range(4):
+        for q in range(QUADRANTS):
             nc.sync.dma_start(
                 out=x_scale_table[32 * q : 32 * q + 8, :].bitcast(I32),
                 in_=x_scales[:, 4 * q : 4 * q + 4, :].bitcast(I32),
             )
-        raw_weights = [load_columns("w1a", w1[0:K_PASS], 0, H)]
+        raw_weights = [load_rows("w1a", w1[0:K_PASS])]
         x_tables.append(load_table(1))
+        raw_weights.append(load_rows("w2a", w2[0:K_PASS]))
+        raw_weights.append(load_rows("w1b", w1[K_PASS:K]))
+        raw_weights.append(load_rows("w2b", w2[K_PASS:K]))
+        raw_w3 = load_rows("w3", w3)
+        raw_edges = [load_rows("e%d" % lo, eT[:, lo : lo + V // 2]) for lo in (0, V // 2)]
         nc.sync.dma_start(out=w4_codes[:].bitcast(I32), in_=w4_words[0].bitcast(I32))
-        for q in range(4):
+        for q in range(QUADRANTS):
             nc.sync.dma_start(
                 out=w4_plane[32 * q : 32 * q + 4, :].bitcast(I32),
                 in_=w4_scales[0, 4 * q : 4 * q + 4, :].bitcast(I32),
             )
-        raw_weights.append(load_columns("w2a", w2[0:K_PASS], 0, H))
-        raw_weights.append(load_columns("w1b", w1[K_PASS:K], 0, H))
-        raw_weights.append(load_columns("w2b", w2[K_PASS:K], 0, H))
-        raw_w3 = load_columns("w3", w3, 0, H)
-        raw_edges = []
-        for lo, hi in E_LOADS:
-            raw = load_columns("e", eT, lo, hi)
-            for v0 in range(lo, hi, CHUNK):
-                raw_edges.append(raw[:, :, v0 - lo : v0 - lo + CHUNK])
 
         x_plane = keep.tile([P, S], U8, name="x_plane", align_bytes=64)
         x_codes = []
-        for z in range(2):
+        for z in range(K // K_PASS):
             picked = keep.tile([P, S], U32, name="x_codes%d" % z, align_bytes=64)
             nc.vector.tensor_copy(picked[:], x_tables[z][:].bitcast(U32).indirect(offsets[:]))
             x_codes.append(picked)
@@ -97,11 +92,14 @@ def tile_picked_edgeup_silu_p_kernel(
         def quantize_weights(name, raw, copies):
             codes = keep.tile([P, H], U32, name=name + "_codes", align_bytes=64)
             plane = keep.tile([P, H], U8, name=name + "_plane", align_bytes=64)
-            src = raw[:].rearrange("p j (m t) -> p m j t", t=PACK)
+            dealt = raw[:].rearrange("p j (m t) -> p m j t", t=PACK)
             stages = []
             for half, copy in enumerate(copies):
                 stage = keep.tile([P, H * PACK // 2], BF16, name="%s_stage%d" % (name, half), align_bytes=64)
-                copy(stage[:].rearrange("p (t m j) -> p m j t", t=PACK, j=PACK), src[:, half * HALF : (half + 1) * HALF])
+                copy(
+                    stage[:].rearrange("p (t m j) -> p m j t", t=PACK, j=PACK),
+                    dealt[:, half * HALF : (half + 1) * HALF],
+                )
                 stages.append(stage)
             for half, stage in enumerate(stages):
                 for t in range(PACK):
@@ -113,67 +111,56 @@ def tile_picked_edgeup_silu_p_kernel(
                     )
             return codes, plane, stages
 
-        def quantize(name, grouped):
-            width = grouped.shape[1] // PACK
-            codes = keep.tile([P, width], U32, name=name + "_codes", align_bytes=64)
-            plane = keep.tile([P, width], U8, name=name + "_plane", align_bytes=64)
-            nc.vector.quantize_mx(out=codes[:].bitcast(FP8X4), scales=plane[:], in_=grouped)
+        def quantize_chunk(name, stage):
+            codes = keep.tile([P, CHUNK], U32, name=name + "_codes", align_bytes=64)
+            plane = keep.tile([P, CHUNK], U8, name=name + "_plane", align_bytes=64)
+            nc.vector.quantize_mx(out=codes[:].bitcast(FP8X4), scales=plane[:], in_=stage)
             return codes, plane
 
-        def add_pass(c, weights, rhs, rhs_scale, first, last):
-            codes, plane = weights[:2]
+        def add_pass(c, w_codes, w_plane, rhs, rhs_scale, first, last):
             for t in range(PACK):
                 cols = slice(t * P, (t + 1) * P)
                 nc.tensor.matmul_mx(
                     out=banks[c][:, t, :],
-                    lhsT=codes[:, cols].bitcast(FP8X4),
-                    lhsT_scale=plane[:, cols],
+                    lhsT=w_codes[:, cols].bitcast(FP8X4),
+                    lhsT_scale=w_plane[:, cols],
                     rhs=rhs.bitcast(FP8X4),
                     rhs_scale=rhs_scale,
                     start=(first and t == 0),
                     stop=(last and t == PACK - 1),
                 )
 
-        shared = (nc.vector.tensor_copy, nc.scalar.copy)
-        scalar_alone = (nc.scalar.copy, nc.scalar.copy)
-        node_weights = []
-        for i in range(4):
+        for i, raw in enumerate(raw_weights):
             z, side = divmod(i, 2)
-            weights = quantize_weights("w%d" % i, raw_weights[i], shared if i > 0 else scalar_alone)
-            node_weights.append(weights)
+            copies = (nc.scalar.copy if i == 0 else nc.vector.tensor_copy, nc.scalar.copy)
+            w_codes, w_plane = quantize_weights("w%d" % i, raw, copies)[:2]
             for c in range(CHUNKS):
                 cols = slice(side * V + c * CHUNK, side * V + (c + 1) * CHUNK)
-                add_pass(c, weights, x_codes[z][:, cols], x_plane[4 * z : P, cols], i == 0, False)
+                add_pass(c, w_codes, w_plane, x_codes[z][:, cols], x_plane[4 * z : P, cols], i == 0, False)
 
-        edge_weights = quantize_weights("w3", raw_w3, shared)
-        w3_stages = edge_weights[2]
-
-        edge_codes = []
+        w3_codes, w3_plane, w3_stages = quantize_weights("w3", raw_w3, (nc.vector.tensor_copy, nc.scalar.copy))
         for c in range(CHUNKS):
-            half, slot = E_SLOTS[c]
-            e_grouped = w3_stages[half][:, slot * CHUNK * PACK : (slot + 1) * CHUNK * PACK]
-            dst = e_grouped.rearrange("p (v i j) -> p v j i", i=PACK, j=PACK)
-            src = raw_edges[c].rearrange("p j (v i) -> p v j i", i=PACK)
-            if c in E_ON_SCALAR:
-                nc.scalar.copy(dst, src)
-            else:
-                nc.vector.tensor_copy(dst, src)
-            e_codes, e_plane = quantize("e%d" % c, e_grouped)
-            edge_codes.append(e_codes)
-            add_pass(c, edge_weights, e_codes[:], e_plane[:], False, True)
+            load, slot = divmod(c, 2)
+            e_stage = w3_stages[0][:, slot * CHUNK * PACK : (slot + 1) * CHUNK * PACK]
+            copy = nc.scalar.copy if c == 1 else nc.vector.tensor_copy
+            copy(
+                e_stage.rearrange("p (v n j) -> p v j n", n=LINE, j=PACK),
+                raw_edges[load][:, :, slot * CHUNK : (slot + 1) * CHUNK].rearrange("p j (v n) -> p v j n", n=LINE),
+            )
+            e_codes, e_plane = quantize_chunk("e%d" % c, e_stage)
+            add_pass(c, w3_codes, w3_plane, e_codes[:], e_plane[:], False, True)
 
         hidden = []
         for c in range(CHUNKS):
-            h_grouped = keep.tile([P, CHUNK * PACK], BF16, name="h_grouped%d" % c, align_bytes=64)
+            h_stage = keep.tile([P, CHUNK * PACK], BF16, name="h_stage%d" % c, align_bytes=64)
             nc.scalar.activation(
-                h_grouped[:].rearrange("p (v t) -> p v t", t=PACK),
+                h_stage[:].rearrange("p (v t) -> p v t", t=PACK),
                 banks[c][:].rearrange("p t v -> p v t"),
                 SILU,
                 bias=silu_bias[:],
             )
-            hidden.append(quantize("h%d" % c, h_grouped[:]))
+            hidden.append(quantize_chunk("h%d" % c, h_stage[:]))
 
-        results = []
         for lo, hi, on_scalar in OUT_GROUPS:
             out_bank = psum.tile([P, (hi - lo) * CHUNK], F32, name="out_bank%d" % lo)
             for c in range(lo, hi):
@@ -188,9 +175,6 @@ def tile_picked_edgeup_silu_p_kernel(
                     stop=True,
                 )
             result = keep.tile([P, (hi - lo) * CHUNK], F32, name="result%d" % lo)
-            if on_scalar:
-                nc.scalar.copy(result[:], out_bank[:])
-            else:
-                nc.vector.tensor_copy(result[:], out_bank[:])
+            copy_out = nc.scalar.copy if on_scalar else nc.vector.tensor_copy
+            copy_out(result[:], out_bank[:])
             nc.sync.dma_start(out=out[:, lo * CHUNK : hi * CHUNK], in_=result[:])
-            results.append(result)

@@ -32,6 +32,7 @@ def tile_picked_edgeup_silu_p_kernel(
     nc = tc.nc
     with ExitStack() as ctx:
         keep = ctx.enter_context(tc.tile_pool(name="keep", bufs=1))
+        reuse = ctx.enter_context(tc.tile_pool(name="reuse", bufs=1))
         psum = ctx.enter_context(tc.psum_pool(name="psum", bufs=1))
 
         def load_table(z):
@@ -44,10 +45,18 @@ def tile_picked_edgeup_silu_p_kernel(
             nc.sync.dma_start(out=raw[:], in_=rows.rearrange("(p j) c -> p j c", j=PACK))
             return raw
 
+        def load_x_scales(rows):
+            for r in rows:
+                for z in range(K // K_PASS):
+                    nc.sync.dma_start(
+                        out=x_scale_table[4 * z + r : P : 32, :].bitcast(I32),
+                        in_=x_scales[z, r : 4 * QUADRANTS : 4, :].bitcast(I32),
+                    )
+
         offsets = keep.tile([P, S // 16], U16, name="offsets")
         nc.sync.dma_start(offsets[:], offs)
 
-        x_scale_table = keep.tile([P, T], U8, name="x_scale_table", align_bytes=64)
+        x_scale_table = reuse.tile([P, T], U8, name="x_scale_table", align_bytes=64, offset=0)
         nc.vector.memset(x_scale_table[:].bitcast(I32), 0)
         w4_codes = keep.tile([P, 2 * N], U8, name="w4_codes", align_bytes=64)
         w4_plane = keep.tile([P, N], U8, name="w4_plane", align_bytes=64)
@@ -59,12 +68,9 @@ def tile_picked_edgeup_silu_p_kernel(
         nc.scalar.activation(silu_bias[:], zero[:], SILU)
 
         x_tables = [load_table(0)]
-        for q in range(QUADRANTS):
-            nc.sync.dma_start(
-                out=x_scale_table[32 * q : 32 * q + 8, :].bitcast(I32),
-                in_=x_scales[:, 4 * q : 4 * q + 4, :].bitcast(I32),
-            )
+        load_x_scales((0, 1))
         raw_weights = [load_rows("w1a", w1[0:K_PASS])]
+        load_x_scales((2, 3))
         x_tables.append(load_table(1))
         raw_weights.append(load_rows("w2a", w2[0:K_PASS]))
         raw_weights.append(load_rows("w1b", w1[K_PASS:K]))
@@ -81,7 +87,10 @@ def tile_picked_edgeup_silu_p_kernel(
         x_plane = keep.tile([P, S], U8, name="x_plane", align_bytes=64)
         x_codes = []
         for z in range(K // K_PASS):
-            picked = keep.tile([P, S], U32, name="x_codes%d" % z, align_bytes=64)
+            if z == 0:
+                picked = keep.tile([P, S], U32, name="x_codes0", align_bytes=64)
+            else:
+                picked = reuse.tile([P, S], U32, name="x_codes1", align_bytes=64, offset=H)
             nc.vector.tensor_copy(picked[:], x_tables[z][:].bitcast(U32).indirect(offsets[:]))
             x_codes.append(picked)
             if z == 0:
@@ -91,7 +100,10 @@ def tile_picked_edgeup_silu_p_kernel(
 
         def quantize_weights(name, raw, copies):
             codes = keep.tile([P, H], U32, name=name + "_codes", align_bytes=64)
-            plane = keep.tile([P, H], U8, name=name + "_plane", align_bytes=64)
+            if name == "w0":
+                plane = reuse.tile([P, H], U8, name=name + "_plane", align_bytes=64, offset=0)
+            else:
+                plane = keep.tile([P, H], U8, name=name + "_plane", align_bytes=64)
             dealt = raw[:].rearrange("p j (m t) -> p m j t", t=PACK)
             stages = []
             for half, copy in enumerate(copies):
@@ -132,7 +144,7 @@ def tile_picked_edgeup_silu_p_kernel(
 
         for i, raw in enumerate(raw_weights):
             z, side = divmod(i, 2)
-            copies = (nc.scalar.copy if i == 0 else nc.vector.tensor_copy, nc.scalar.copy)
+            copies = (nc.scalar.copy if i < 2 else nc.vector.tensor_copy, nc.scalar.copy)
             w_codes, w_plane = quantize_weights("w%d" % i, raw, copies)[:2]
             for c in range(CHUNKS):
                 cols = slice(side * V + c * CHUNK, side * V + (c + 1) * CHUNK)

@@ -24,6 +24,21 @@ CHUNKS = V // CHUNK
 LINE = 4
 HALF = P // 2
 OUT_GROUPS = ((0, 2, False), (2, 3, False), (3, 4, True))
+KIB = 1024
+PLACES = {
+    "x_table0": 8 * KIB,
+    "w1b_raw": 4 * KIB,
+    "w2b_raw": 12 * KIB,
+    "x_scale_table": 20 * KIB,
+    "x_codes0": 20 * KIB,
+    "w1a_raw": 24 * KIB,
+    "w3_raw": 24 * KIB,
+    "w2a_raw": 32 * KIB,
+    "e0_raw": 32 * KIB,
+    "e1_raw": 36 * KIB,
+    "w4_codes": 4 * KIB,
+    "w4_plane": 5 * KIB,
+}
 
 
 def tile_picked_edgeup_silu_p_kernel(
@@ -35,32 +50,23 @@ def tile_picked_edgeup_silu_p_kernel(
         reuse = ctx.enter_context(tc.tile_pool(name="reuse", bufs=1))
         psum = ctx.enter_context(tc.psum_pool(name="psum", bufs=1))
 
+        def place(name, shape, dtype):
+            if name in PLACES:
+                return reuse.tile(shape, dtype, name=name, align_bytes=64, offset=PLACES[name])
+            return keep.tile(shape, dtype, name=name, align_bytes=64)
+
         def load_table(z):
-            table = keep.tile([P, T], I32, name="x_table%d" % z, align_bytes=64)
+            table = place("x_table%d" % z, [P, T], I32)
             nc.sync.dma_start(out=table[:], in_=x_words[z].rearrange("p n t -> p (n t)").bitcast(I32))
             return table
 
         def load_rows(name, rows):
-            raw = keep.tile([P, PACK, rows.shape[1]], F32, name=name + "_raw")
+            raw = place(name + "_raw", [P, PACK, rows.shape[1]], F32)
             nc.sync.dma_start(out=raw[:], in_=rows.rearrange("(p j) c -> p j c", j=PACK))
             return raw
 
-        def load_x_scales(rows):
-            for r in rows:
-                for z in range(K // K_PASS):
-                    nc.sync.dma_start(
-                        out=x_scale_table[4 * z + r : P : 32, :].bitcast(I32),
-                        in_=x_scales[z, r : 4 * QUADRANTS : 4, :].bitcast(I32),
-                    )
-
-        offsets = keep.tile([P, S // 16], U16, name="offsets")
-        nc.sync.dma_start(offsets[:], offs)
-
-        x_scale_table = reuse.tile([P, T], U8, name="x_scale_table", align_bytes=64, offset=0)
+        x_scale_table = place("x_scale_table", [P, T], U8)
         nc.vector.memset(x_scale_table[:].bitcast(I32), 0)
-        w4_codes = keep.tile([P, 2 * N], U8, name="w4_codes", align_bytes=64)
-        w4_plane = keep.tile([P, N], U8, name="w4_plane", align_bytes=64)
-        nc.vector.memset(w4_plane[:].bitcast(I32), 0)
 
         zero = keep.tile([P, 1], F32, name="zero")
         nc.vector.memset(zero[:], 0.0)
@@ -68,42 +74,38 @@ def tile_picked_edgeup_silu_p_kernel(
         nc.scalar.activation(silu_bias[:], zero[:], SILU)
 
         x_tables = [load_table(0)]
-        load_x_scales((0, 1))
+        offsets = keep.tile([P, S // 16], U16, name="offsets")
+        nc.sync.dma_start(offsets[:], offs)
+        for z in range(K // K_PASS):
+            nc.sync.dma_start(out=x_scale_table[4 * z : P : 8, :].bitcast(I32), in_=x_scales[z].bitcast(I32))
         raw_weights = [load_rows("w1a", w1[0:K_PASS])]
-        load_x_scales((2, 3))
         x_tables.append(load_table(1))
         raw_weights.append(load_rows("w2a", w2[0:K_PASS]))
-        raw_weights.append(load_rows("w1b", w1[K_PASS:K]))
-        raw_weights.append(load_rows("w2b", w2[K_PASS:K]))
-        raw_w3 = load_rows("w3", w3)
-        raw_edges = [load_rows("e%d" % lo, eT[:, lo : lo + V // 2]) for lo in (0, V // 2)]
-        nc.sync.dma_start(out=w4_codes[:].bitcast(I32), in_=w4_words[0].bitcast(I32))
-        for q in range(QUADRANTS):
-            nc.sync.dma_start(
-                out=w4_plane[32 * q : 32 * q + 4, :].bitcast(I32),
-                in_=w4_scales[0, 4 * q : 4 * q + 4, :].bitcast(I32),
-            )
 
+        x_scale_picked = keep.tile([P, S], U8, name="x_scale_picked", align_bytes=64)
+        nc.vector.tensor_copy(x_scale_picked[:], x_scale_table[:].indirect(offsets[:]))
         x_plane = keep.tile([P, S], U8, name="x_plane", align_bytes=64)
+        nc.vector.tensor_copy(x_plane[:].bitcast(I32), x_scale_picked[:].bitcast(I32))
+        for r in range(1, 4):
+            for z in range(K // K_PASS):
+                nc.sync.dma_start(
+                    out=x_plane[4 * z + r : P : 32, :].bitcast(I32),
+                    in_=x_scale_picked[8 * r + 4 * z : P : 32, :].bitcast(I32),
+                )
+
         x_codes = []
         for z in range(K // K_PASS):
-            if z == 0:
-                picked = keep.tile([P, S], U32, name="x_codes0", align_bytes=64)
-            else:
-                picked = reuse.tile([P, S], U32, name="x_codes1", align_bytes=64, offset=H)
+            picked = place("x_codes%d" % z, [P, S], U32)
             nc.vector.tensor_copy(picked[:], x_tables[z][:].bitcast(U32).indirect(offsets[:]))
             x_codes.append(picked)
-            if z == 0:
-                nc.vector.tensor_copy(x_plane[:], x_scale_table[:].indirect(offsets[:]))
+        raw_weights.append(load_rows("w1b", w1[K_PASS:K]))
+        raw_weights.append(load_rows("w2b", w2[K_PASS:K]))
 
         banks = [psum.tile([P, PACK, CHUNK], F32, name="h_bank%d" % c) for c in range(CHUNKS)]
 
         def quantize_weights(name, raw, copies):
             codes = keep.tile([P, H], U32, name=name + "_codes", align_bytes=64)
-            if name == "w0":
-                plane = reuse.tile([P, H], U8, name=name + "_plane", align_bytes=64, offset=0)
-            else:
-                plane = keep.tile([P, H], U8, name=name + "_plane", align_bytes=64)
+            plane = keep.tile([P, H], U8, name=name + "_plane", align_bytes=64)
             dealt = raw[:].rearrange("p j (m t) -> p m j t", t=PACK)
             stages = []
             for half, copy in enumerate(copies):
@@ -145,7 +147,21 @@ def tile_picked_edgeup_silu_p_kernel(
         for i, raw in enumerate(raw_weights):
             z, side = divmod(i, 2)
             copies = (nc.scalar.copy if i < 2 else nc.vector.tensor_copy, nc.scalar.copy)
-            w_codes, w_plane = quantize_weights("w%d" % i, raw, copies)[:2]
+            w_codes, w_plane = quantize_weights("node%d" % i, raw, copies)[:2]
+            if i == 0:
+                raw_w3 = load_rows("w3", w3)
+            if i == 1:
+                raw_edges = [load_rows("e%d" % h, eT[:, h * V // 2 : (h + 1) * V // 2]) for h in range(2)]
+            if i == 2:
+                w4_codes = place("w4_codes", [P, 2 * N], U8)
+                w4_plane = place("w4_plane", [P, N], U8)
+                nc.vector.memset(w4_plane[:].bitcast(I32), 0)
+                nc.sync.dma_start(out=w4_codes[:].bitcast(I32), in_=w4_words[0].bitcast(I32))
+                for q in range(QUADRANTS):
+                    nc.sync.dma_start(
+                        out=w4_plane[32 * q : 32 * q + 4, :].bitcast(I32),
+                        in_=w4_scales[0, 4 * q : 4 * q + 4, :].bitcast(I32),
+                    )
             for c in range(CHUNKS):
                 cols = slice(side * V + c * CHUNK, side * V + (c + 1) * CHUNK)
                 add_pass(c, w_codes, w_plane, x_codes[z][:, cols], x_plane[4 * z : P, cols], i == 0, False)

@@ -27,8 +27,8 @@ OUT_GROUPS = ((0, 2, False), (2, 3, False), (3, 4, True))
 KIB = 1024
 PLACES = {
     "x_table0": 8 * KIB,
-    "w1b_raw": 4 * KIB,
-    "w2b_raw": 12 * KIB,
+    "w1b_raw": 0,
+    "w2b_raw": 8 * KIB,
     "x_scale_table": 20 * KIB,
     "x_codes0": 20 * KIB,
     "w1a_raw": 24 * KIB,
@@ -81,6 +81,7 @@ def tile_picked_edgeup_silu_p_kernel(
         raw_weights = [load_rows("w1a", w1[0:K_PASS])]
         x_tables.append(load_table(1))
         raw_weights.append(load_rows("w2a", w2[0:K_PASS]))
+        raw_weights.append(load_rows("w1b", w1[K_PASS:K]))
 
         x_scale_picked = keep.tile([P, S], U8, name="x_scale_picked", align_bytes=64)
         nc.vector.tensor_copy(x_scale_picked[:], x_scale_table[:].indirect(offsets[:]))
@@ -98,7 +99,6 @@ def tile_picked_edgeup_silu_p_kernel(
             picked = place("x_codes%d" % z, [P, S], U32)
             nc.vector.tensor_copy(picked[:], x_tables[z][:].bitcast(U32).indirect(offsets[:]))
             x_codes.append(picked)
-        raw_weights.append(load_rows("w1b", w1[K_PASS:K]))
         raw_weights.append(load_rows("w2b", w2[K_PASS:K]))
 
         banks = [psum.tile([P, PACK, CHUNK], F32, name="h_bank%d" % c) for c in range(CHUNKS)]

@@ -85,14 +85,16 @@ def tile_picked_edgeup_silu_p_kernel(
 
         x_scale_picked = keep.tile([P, S], U8, name="x_scale_picked", align_bytes=64)
         nc.vector.tensor_copy(x_scale_picked[:], x_scale_table[:].indirect(offsets[:]))
-        x_plane = keep.tile([P, S], U8, name="x_plane", align_bytes=64)
-        nc.vector.tensor_copy(x_plane[:].bitcast(I32), x_scale_picked[:].bitcast(I32))
-        for r in range(1, 4):
-            for z in range(K // K_PASS):
-                nc.sync.dma_start(
-                    out=x_plane[4 * z + r : P : 32, :].bitcast(I32),
+        x_planes = []
+        for z, queue in enumerate((nc.sync, nc.gpsimd)):
+            plane = keep.tile([P, S], U8, name="x_plane%d" % z, align_bytes=64)
+            nc.vector.tensor_copy(plane[:].bitcast(I32), x_scale_picked[:].bitcast(I32))
+            for r in range(1, 4):
+                queue.dma_start(
+                    out=plane[4 * z + r : P : 32, :].bitcast(I32),
                     in_=x_scale_picked[8 * r + 4 * z : P : 32, :].bitcast(I32),
                 )
+            x_planes.append(plane)
 
         x_codes = []
         for z in range(K // K_PASS):
@@ -164,7 +166,7 @@ def tile_picked_edgeup_silu_p_kernel(
                     )
             for c in range(CHUNKS):
                 cols = slice(side * V + c * CHUNK, side * V + (c + 1) * CHUNK)
-                add_pass(c, w_codes, w_plane, x_codes[z][:, cols], x_plane[4 * z : P, cols], i == 0, False)
+                add_pass(c, w_codes, w_plane, x_codes[z][:, cols], x_planes[z][4 * z : P, cols], i == 0, False)
 
         w3_codes, w3_plane, w3_stages = quantize_weights("w3", raw_w3, (nc.vector.tensor_copy, nc.scalar.copy))
         for c in range(CHUNKS):

@@ -168,10 +168,11 @@ def tile_picked_edgeup_silu_p_kernel(
                 cols = slice(side * V + c * CHUNK, side * V + (c + 1) * CHUNK)
                 add_pass(c, w_codes, w_plane, x_codes[z][:, cols], x_planes[z][4 * z : P, cols], i == 0, False)
 
-        w3_codes, w3_plane, w3_stages = quantize_weights("w3", raw_w3, (nc.vector.tensor_copy, nc.scalar.copy))
+        w3_codes, w3_plane = quantize_weights("w3", raw_w3, (nc.vector.tensor_copy, nc.scalar.copy))[:2]
+        e_stages = keep.tile([P, 3, CHUNK * PACK], BF16, name="e_stages", align_bytes=64)
         for c in range(CHUNKS):
             load, slot = divmod(c, 2)
-            e_stage = w3_stages[0][:, slot * CHUNK * PACK : (slot + 1) * CHUNK * PACK]
+            e_stage = e_stages[:, c if c < 3 else 1, :]
             copy = nc.scalar.copy if c == 1 else nc.vector.tensor_copy
             copy(
                 e_stage.rearrange("p (v n j) -> p v j n", n=LINE, j=PACK),

from contextlib import ExitStack

import concourse.mybir as mybir

K, T, S, V, H, N, J = 1024, 2048, 1024, 512, 512, 128, 512
FLOPS = 2 * (2 * K * H * V + J * H * V + H * N * V)

F32 = mybir.dt.float32
BF16 = mybir.dt.bfloat16
I32 = mybir.dt.int32
U32 = mybir.dt.uint32
U16 = mybir.dt.uint16
U8 = mybir.dt.uint8
FP8X4 = mybir.dt.float8_e4m3fn_x4
FP4X4 = mybir.dt.float4_e2m1fn_x4
SILU = mybir.ActivationFunctionType.Silu

P = 128
PACK = 4
K_PASS = P * PACK
QUADRANTS = 4
CHUNK = 128
CHUNKS = V // CHUNK
LINE = 4
HALF = P // 2
OUT_GROUPS = ((0, 2, False), (2, 3, False), (3, 4, True))
KIB = 1024
PLACES = {
    "x_table0": 8 * KIB,
    "w1b_raw": 0,
    "w2b_raw": 8 * KIB,
    "x_scale_table": 20 * KIB,
    "x_codes0": 20 * KIB,
    "w1a_raw": 24 * KIB,
    "w3_raw": 24 * KIB,
    "w2a_raw": 32 * KIB,
    "e0_raw": 32 * KIB,
    "e1_raw": 36 * KIB,
    "w4_codes": 4 * KIB,
    "w4_plane": 5 * KIB,
}


def tile_picked_edgeup_silu_p_kernel(
    tc, x_words, x_scales, eT, w1, w2, w3, w4_words, w4_scales, offs, out
):
    nc = tc.nc
    with ExitStack() as ctx:
        keep = ctx.enter_context(tc.tile_pool(name="keep", bufs=1))
        reuse = ctx.enter_context(tc.tile_pool(name="reuse", bufs=1))
        psum = ctx.enter_context(tc.psum_pool(name="psum", bufs=1))

        def place(name, shape, dtype):
            if name in PLACES:
                return reuse.tile(shape, dtype, name=name, align_bytes=64, offset=PLACES[name])
            return keep.tile(shape, dtype, name=name, align_bytes=64)

        def load_table(z):
            table = place("x_table%d" % z, [P, T], I32)
            nc.sync.dma_start(out=table[:], in_=x_words[z].rearrange("p n t -> p (n t)").bitcast(I32))
            return table

        def load_rows(name, rows):
            raw = place(name + "_raw", [P, PACK, rows.shape[1]], F32)
            nc.sync.dma_start(out=raw[:], in_=rows.rearrange("(p j) c -> p j c", j=PACK))
            return raw

        x_scale_table = place("x_scale_table", [P, T], U8)
        nc.vector.memset(x_scale_table[:].bitcast(I32), 0)

        zero = keep.tile([P, 1], F32, name="zero")
        nc.vector.memset(zero[:], 0.0)
        silu_bias = keep.tile([P, 1], F32, name="silu_bias")
        nc.scalar.activation(silu_bias[:], zero[:], SILU)

        x_tables = [load_table(0)]
        offsets = keep.tile([P, S // 16], U16, name="offsets")
        nc.sync.dma_start(offsets[:], offs)
        for z in range(K // K_PASS):
            nc.sync.dma_start(out=x_scale_table[4 * z : P : 8, :].bitcast(I32), in_=x_scales[z].bitcast(I32))
        raw_weights = [load_rows("w1a", w1[0:K_PASS])]
        x_tables.append(load_table(1))
        raw_weights.append(load_rows("w2a", w2[0:K_PASS]))
        raw_weights.append(load_rows("w1b", w1[K_PASS:K]))

        x_scale_picked = keep.tile([P, S], U8, name="x_scale_picked", align_bytes=64)
        nc.vector.tensor_copy(x_scale_picked[:], x_scale_table[:].indirect(offsets[:]))
        x_planes = []
        for z, queue in enumerate((nc.sync, nc.gpsimd)):
            plane = keep.tile([P, S], U8, name="x_plane%d" % z, align_bytes=64)
            nc.vector.tensor_copy(plane[:].bitcast(I32), x_scale_picked[:].bitcast(I32))
            for r in range(1, 4):
                queue.dma_start(
                    out=plane[4 * z + r : P : 32, :].bitcast(I32),
                    in_=x_scale_picked[8 * r + 4 * z : P : 32, :].bitcast(I32),
                )
            x_planes.append(plane)

        x_codes = []
        for z in range(K // K_PASS):
            picked = place("x_codes%d" % z, [P, S], U32)
            nc.vector.tensor_copy(picked[:], x_tables[z][:].bitcast(U32).indirect(offsets[:]))
            x_codes.append(picked)
        raw_weights.append(load_rows("w2b", w2[K_PASS:K]))

        banks = [psum.tile([P, PACK, CHUNK], F32, name="h_bank%d" % c) for c in range(CHUNKS)]

        def quantize_weights(name, raw, copies):
            codes = keep.tile([P, H], U32, name=name + "_codes", align_bytes=64)
            plane = keep.tile([P, H], U8, name=name + "_plane", align_bytes=64)
            dealt = raw[:].rearrange("p j (m t) -> p m j t", t=PACK)
            stages = []
            for half, copy in enumerate(copies):
                stage = keep.tile([P, H * PACK // 2], BF16, name="%s_stage%d" % (name, half), align_bytes=64)
                copy(
                    stage[:].rearrange("p (t m j) -> p m j t", t=PACK, j=PACK),
                    dealt[:, half * HALF : (half + 1) * HALF],
                )
                stages.append(stage)
            for half, stage in enumerate(stages):
                for t in range(PACK):
                    cols = slice(t * P + half * HALF, t * P + (half + 1) * HALF)
                    nc.vector.quantize_mx(
                        out=codes[:, cols].bitcast(FP8X4),
                        scales=plane[:, cols],
                        in_=stage[:, t * HALF * PACK : (t + 1) * HALF * PACK],
                    )
            return codes, plane, stages

        def quantize_chunk(name, stage):
            codes = keep.tile([P, CHUNK], U32, name=name + "_codes", align_bytes=64)
            plane = keep.tile([P, CHUNK], U8, name=name + "_plane", align_bytes=64)
            nc.vector.quantize_mx(out=codes[:].bitcast(FP8X4), scales=plane[:], in_=stage)
            return codes, plane

        def add_pass(c, w_codes, w_plane, rhs, rhs_scale, first, last):
            for t in range(PACK):
                cols = slice(t * P, (t + 1) * P)
                nc.tensor.matmul_mx(
                    out=banks[c][:, t, :],
                    lhsT=w_codes[:, cols].bitcast(FP8X4),
                    lhsT_scale=w_plane[:, cols],
                    rhs=rhs.bitcast(FP8X4),
                    rhs_scale=rhs_scale,
                    start=(first and t == 0),
                    stop=(last and t == PACK - 1),
                )

        for i, raw in enumerate(raw_weights):
            z, side = divmod(i, 2)
            copies = (nc.scalar.copy if i < 2 else nc.vector.tensor_copy, nc.scalar.copy)
            w_codes, w_plane = quantize_weights("node%d" % i, raw, copies)[:2]
            if i == 0:
                raw_w3 = load_rows("w3", w3)
            if i == 1:
                raw_edges = [load_rows("e%d" % h, eT[:, h * V // 2 : (h + 1) * V // 2]) for h in range(2)]
            if i == 2:
                w4_codes = place("w4_codes", [P, 2 * N], U8)
                w4_plane = place("w4_plane", [P, N], U8)
                nc.vector.memset(w4_plane[:].bitcast(I32), 0)
                nc.sync.dma_start(out=w4_codes[:].bitcast(I32), in_=w4_words[0].bitcast(I32))
                for q in range(QUADRANTS):
                    nc.sync.dma_start(
                        out=w4_plane[32 * q : 32 * q + 4, :].bitcast(I32),
                        in_=w4_scales[0, 4 * q : 4 * q + 4, :].bitcast(I32),
                    )
            for c in range(CHUNKS):
                cols = slice(side * V + c * CHUNK, side * V + (c + 1) * CHUNK)
                add_pass(c, w_codes, w_plane, x_codes[z][:, cols], x_planes[z][4 * z : P, cols], i == 0, False)

        w3_codes, w3_plane = quantize_weights("w3", raw_w3, (nc.vector.tensor_copy, nc.scalar.copy))[:2]
        e_stages = keep.tile([P, 3, CHUNK * PACK], BF16, name="e_stages", align_bytes=64)
        for c in range(CHUNKS):
            load, slot = divmod(c, 2)
            e_stage = e_stages[:, c if c < 3 else 1, :]
            copy = nc.scalar.copy if c == 1 else nc.vector.tensor_copy
            copy(
                e_stage.rearrange("p (v n j) -> p v j n", n=LINE, j=PACK),
                raw_edges[load][:, :, slot * CHUNK : (slot + 1) * CHUNK].rearrange("p j (v n) -> p v j n", n=LINE),
            )
            e_codes, e_plane = quantize_chunk("e%d" % c, e_stage)
            add_pass(c, w3_codes, w3_plane, e_codes[:], e_plane[:], False, True)

        hidden = []
        for c in range(CHUNKS):
            h_stage = keep.tile([P, CHUNK * PACK], BF16, name="h_stage%d" % c, align_bytes=64)
            nc.scalar.activation(
                h_stage[:].rearrange("p (v t) -> p v t", t=PACK),
                banks[c][:].rearrange("p t v -> p v t"),
                SILU,
                bias=silu_bias[:],
            )
            hidden.append(quantize_chunk("h%d" % c, h_stage[:]))

        for lo, hi, on_scalar in OUT_GROUPS:
            out_bank = psum.tile([P, (hi - lo) * CHUNK], F32, name="out_bank%d" % lo)
            for c in range(lo, hi):
                h_codes, h_plane = hidden[c]
                nc.tensor.matmul_mx(
                    out=out_bank[:, (c - lo) * CHUNK : (c - lo + 1) * CHUNK],
                    lhsT=w4_codes[:].bitcast(FP4X4),
                    lhsT_scale=w4_plane[:],
                    rhs=h_codes[:].bitcast(FP8X4),
                    rhs_scale=h_plane[:],
                    start=True,
                    stop=True,
                )
            result = keep.tile([P, (hi - lo) * CHUNK], F32, name="result%d" % lo)
            copy_out = nc.scalar.copy if on_scalar else nc.vector.tensor_copy
            copy_out(result[:], out_bank[:])
            nc.sync.dma_start(out=out[:, lo * CHUNK : hi * CHUNK], in_=result[:])
